import numpy as np
CORES = [97,101,225,229,353,357,481,485]
N = 8
T, G, CAP = 2048, 2048, 512
def entries(a): return a.T.reshape(-1)
def pack(v, P): return np.ascontiguousarray(np.asarray(v, np.int32).reshape(-1, P).T)
def lists(rng, how):
    S = rng.integers(0, T, (N, 2 * CAP)); P = np.stack([rng.permutation(G)[:2 * CAP] for r in range(N)])
    if how == "alike": S[:] = rng.integers(0, T, (N, 1))
    if how == "edge":
        S = np.where(rng.random((N, 2 * CAP)) < 0.5, 0, T - 1); S[:, [0, CAP]] = 0; S[:, [1, CAP + 1]] = T - 1
        P[:, 1:-1] = np.stack([1 + rng.permutation(G - 2)[:2 * CAP - 2] for r in range(N)]); P[0::2, 0], P[0::2, -1] = 0, G - 1; P[1::2, 0], P[1::2, -1] = G - 1, 0
    if how == "mixed": P = np.stack([rng.permutation(2 * CAP) for r in range(N)]); P[1::2] += G - 2 * CAP
    if how == "sorted":
        S2, P2 = [-np.sort(-A.reshape(N, 2, CAP), axis=2).reshape(N, 2 * CAP) for A in (S, P)]; S, P = -np.sort(-S, axis=1), -np.sort(-P, axis=1)
        S[1::3], P[1::3] = S[1::3, ::-1].copy(), P[1::3, ::-1].copy(); S[2::3], P[2::3] = S2[2::3], P2[2::3]
    return {"snd": np.stack([pack(s, 16) for s in S]), "plc": np.stack([pack(q, 16) for q in P])}
def setup_inputs(rng):
    return dict({"x": rng.standard_normal((N, 128, T), dtype=np.float32), "gh": rng.standard_normal((N, 128, G), dtype=np.float32)}, **lists(rng, "uniform"))
def setup_inputs_alike(rng):
    d = setup_inputs(rng); d.update(lists(rng, "alike"))
    for k in ("x", "gh"): d[k] = (d[k].astype(np.float32) * 1048576.0).astype(d[k].dtype)
    return d
def setup_inputs_edge(rng):
    d = setup_inputs(rng); d.update(lists(rng, "edge"))
    for k in ("x", "gh"): d[k] = (d[k].astype(np.float32) * (1 / 1024.0)).astype(d[k].dtype)
    return d
def setup_inputs_mixed(rng):
    d = setup_inputs(rng); d.update(lists(rng, "mixed"))
    return d
def setup_inputs_sorted(rng):
    d = setup_inputs(rng); d.update(lists(rng, "sorted"))
    return d
def setup_inputs_zeros(rng):
    d = setup_inputs(rng); d.update(lists(rng, "zeros"))
    for r in range(N): d["x"][r][:, entries(d["snd"][r])[::2]] = 0
    return d
def check_inputs(x):
    bad = []
    if x["snd"].min() < 0 or x["snd"].max() >= T: bad.append("snd out of range")
    if x["plc"].min() < 0 or x["plc"].max() >= G: bad.append("plc out of range")
    if any(len(np.unique(a)) != a.size for a in x["plc"]): bad.append("a place is named twice")
    return bad
def reference(x, gh, snd, plc):
    y = gh.copy()
    for r in range(N):
        S = entries(snd[r]); lo, hi = (r - 1) % N, (r + 1) % N
        y[lo][:, entries(plc[lo])[CAP:]] = x[r][:, S[:CAP]]
        y[hi][:, entries(plc[hi])[:CAP]] = x[r][:, S[CAP:]]
    return {"y": y}

@@ -1,0 +1,180 @@
+from concourse.mybir import AluOpType as A, ActivationFunctionType as F, AxisListType
+
+CAP, TC, GC = 512, 2048, 2048
+HALF = CAP // 2
+SPLIT = 384
+
+SCRATCH = {
+    "xs": ("sbuf", [128, TC], "float32"),
+    "w": ("sbuf", [128, GC + 2 * CAP], "float32"),
+    "ys": ("sbuf", [128, GC], "float32"),
+    "sb": ("sbuf", [128, 2 * CAP], "float32"),
+    "negz": ("sbuf", [128, 4], "float32"),
+    "sndi": ("sbuf", [16, 64], "int32"),
+    "sndf": ("sbuf", [16, 64], "float32"),
+    "dq": ("sbuf", [16, 128], "float32"),
+    "rep": ("sbuf", [16, 128], "float32"),
+    "so": ("sbuf", [128, 64], "uint16"),
+    "pli": ("sbuf", [128, 8], "int32"),
+    "kki": ("sbuf", [128, 8], "int32"),
+    "qqi": ("sbuf", [128, 8], "int32"),
+    "kkf": ("sbuf", [128, 8], "float32"),
+    "qqf": ("sbuf", [128, 8], "float32"),
+    "ip": ("sbuf", [128, 8], "int32"),
+    "ip3": ("sbuf", [128, 8], "int32"),
+    "ip15": ("sbuf", [128, 8], "int32"),
+    "p15": ("sbuf", [128, 8], "float32"),
+    "jbase": ("sbuf", [128, 8], "float32"),
+    "jm": ("sbuf", [128, 8], "float32"),
+    "jw": ("sbuf", [128, 8], "float32"),
+    "iok": ("sbuf", [128, 128], "bfloat16"),
+    "ioq": ("sbuf", [128, 128], "bfloat16"),
+    "io16": ("sbuf", [128, 128], "float32"),
+    "mm": ("sbuf", [128, 128], "float32"),
+    "ohq": ("sbuf", [128, 1024], "float16"),
+    "ohk": ("sbuf", [128, 1024], "float16"),
+    "t1": ("sbuf", [128, 128], "float32"),
+    "t2": ("sbuf", [128, 128], "float32"),
+    "t3": ("sbuf", [128, 128], "float32"),
+    "off": ("sbuf", [128, 128], "uint16"),
+    "psa": ("psum", [128, 512], "float32"),
+    "psb": ("psum", [128, 512], "float32"),
+}
+SEMAPHORES = ["lsnd", "lx", "lplc", "lgh", "i1", "i2", "v", "bz", "rr", "pa", "sos", "gf", "gn", "oh", "pb", "offs",
+              "sent", "afar", "anear", "yv1", "ys1", "yv2", "ys2", "st", "st2"]
+
+
+def rank_program(g, core, T, topo):
+    rank = T.rank_of(core)
+    if rank is None:
+        return
+    n = len(T.cores)
+    lo, hi = T.cores[(rank - 1) % n], T.cores[(rank + 1) % n]
+
+    def here(c):
+        return topo.host(c) == topo.host(core) and topo.chip(c) == topo.chip(core)
+
+    near, far = (lo, hi) if here(lo) else (hi, lo)
+    s = T.sem
+    V, S, P, Y = g.vector, g.scalar, g.tensor, g.sync
+
+    def half(dst):
+        return 0 if dst == lo else 1
+
+    def slot(dst):
+        return GC + CAP if dst == lo else GC
+
+    far_mask = topo.mask(core, far)
+    near_mask = topo.mask(core, near) & ~far_mask
+    n_far, n_near = bin(far_mask).count("1"), bin(near_mask).count("1")
+
+    Y.dma_start(T.sndi[:], T.snd[:]).then_inc(s.lsnd, 16)
+    Y.dma_start(T.xs[:], T.x[:]).then_inc(s.lx, 16)
+    Y.dma_start(T.pli[:], T.plc[:]).then_inc(s.lplc, 16)
+    Y.dma_start(T.w[:, 0:GC], T.gh[:]).then_inc(s.lgh, 16)
+
+    g.iota(T.dq[:], [[0, 8], [1, 16]], 0, -1, allow_small_or_imprecise_dtypes=True).then_inc(s.i1, 1)
+    g.iota(T.ip[:], [[0, 8]], 0, 1).then_inc(s.i2, 1)
+    g.iota(T.jbase[:], [[16, 8]], 1, 128, allow_small_or_imprecise_dtypes=True).then_inc(s.i2, 1)
+    g.iota(T.io16[:], [[16, 128]], 0, 0, allow_small_or_imprecise_dtypes=True).then_inc(s.i2, 1)
+    g.iota(T.iok[:], [[1, 128]], 0, 0, allow_small_or_imprecise_dtypes=True).then_inc(s.i2, 1)
+    g.iota(T.ioq[:], [[0, 8], [1, 16]], 0, 0, allow_small_or_imprecise_dtypes=True).then_inc(s.i2, 1)
+
+    nv = [0]
+
+    def v(ins):
+        ins.then_inc(s.v, 1)
+        nv[0] += 1
+
+    def vw():
+        V.wait_ge(s.v, nv[0])
+
+    V.memset(T.negz[:], -0.0).then_inc(s.bz, 1)
+    V.wait_ge(s.i1, 1)
+    V.tensor_scalar(T.rep[:], T.dq[:], 0.0, None, A.is_equal).then_inc(s.rr, 1)
+    V.wait_ge(s.i2, 5)
+    v(V.tensor_scalar(T.ip3[:], T.ip[:], 3, None, A.arith_shift_right))
+    v(V.tensor_scalar(T.ip15[:], T.ip[:], 15, None, A.bitwise_and))
+    vw()
+    v(V.tensor_scalar(T.jm[:], T.ip3[:], -1023.0, None, A.mult))
+    v(V.tensor_copy(T.p15[:], T.ip15[:]))
+    vw()
+    v(V.tensor_tensor(T.jw[:], T.jbase[:], T.jm[:], A.add))
+    v(V.tensor_scalar(T.mm[:], T.io16[:], T.p15[:, 0:1], None, A.add))
+    V.wait_ge(s.lsnd, 16)
+    V.tensor_copy(T.sndf[:], T.sndi[:]).then_inc(s.rr, 1)
+
+    P.wait_ge(s.rr, 2)
+    P.matmul(T.psa[:, 0:64], T.rep[:], T.sndf[:], True, True).then_inc(s.pa, 1)
+
+    V.wait_ge(s.pa, 1)
+    V.tensor_copy(T.so[:], T.psa[:, 0:64]).then_inc(s.sos, 1)
+    V.wait_ge(s.sos, 1)
+    V.wait_ge(s.lx, 16)
+    S.wait_ge(s.bz, 1)
+    S.wait_ge(s.sos, 1)
+    S.wait_ge(s.lx, 16)
+
+    def gather_v(out, win, off, sem):
+        V.tensor_copy(out, win.indirect(off)).then_inc(sem, 1)
+
+    def gather_s(out, win, off, sem):
+        S.activation(out, win.indirect(off), F.Identity, bias=T.negz[:, 0:1]).then_inc(sem, 1)
+
+    for dst, base, sem in ((far, 0, s.gf), (near, CAP, s.gn)):
+        o = 32 * half(dst)
+        gather_v(T.sb[:, base:base + HALF], T.xs[:], T.so[:, o:o + 16], sem)
+        gather_s(T.sb[:, base + HALF:base + CAP], T.xs[:], T.so[:, o + 16:o + 32], sem)
+
+    for dst, base, sem, mask, arr in ((far, 0, s.gf, far_mask, s.afar), (near, CAP, s.gn, near_mask, s.anear)):
+        rid, pid = topo.addr(dst, core)
+        g.wait_ge(sem, 2)
+        g.remote_dma(T.w[:, slot(dst):slot(dst) + CAP], T.sb[:, base:base + CAP], arr, s.sent, pid, rid, mask)
+    g.wait_ge(s.sent, n_far + n_near)
+
+    V.wait_ge(s.lplc, 16)
+    v(V.tensor_scalar(T.kki[:], T.pli[:], 4, None, A.arith_shift_right))
+    v(V.tensor_scalar(T.qqi[:], T.pli[:], 15, None, A.bitwise_and))
+    vw()
+    v(V.tensor_copy(T.kkf[:], T.kki[:]))
+    v(V.tensor_copy(T.qqf[:], T.qqi[:]))
+    vw()
+    for c in range(8):
+        b = slice(128 * c, 128 * c + 128)
+        V.tensor_scalar(T.ohq[:, b], T.ioq[:], T.qqf[:, c:c + 1], None, A.is_equal).then_inc(s.oh, 1)
+        V.tensor_scalar(T.ohk[:, b], T.iok[:], T.kkf[:, c:c + 1], T.jw[:, c:c + 1], A.is_equal, A.mult).then_inc(s.oh, 1)
+    P.wait_ge(s.oh, 16)
+    for c in range(8):
+        b = slice(128 * c, 128 * c + 128)
+        ins = P.matmul(T.psb[:, 0:128], T.ohq[:, b], T.ohk[:, b], c == 0, c == 7)
+    ins.then_inc(s.pb, 1)
+    V.wait_ge(s.pb, 1)
+    v(V.tensor_scalar(T.t1[:], T.psb[:, 0:128], 0.0, 2047.0, A.is_gt, A.mult))
+    vw()
+    v(V.tensor_tensor(T.t2[:], T.t1[:], T.mm[:], A.max))
+    vw()
+    v(V.tensor_tensor(T.t3[:], T.t2[:], T.psb[:, 0:128], A.add))
+    vw()
+    V.tensor_copy(T.off[:], T.t3[:]).then_inc(s.offs, 1)
+
+    for q in (V, S):
+        q.wait_ge(s.offs, 1)
+        q.wait_ge(s.lgh, 16)
+        q.wait_ge(s.anear, n_near)
+        q.wait_ge(s.afar, n_far)
+
+    def block(f, a, b, sem):
+        f(T.ys[:, a:b], T.w[:], T.off[:, a // 16:b // 16], sem)
+
+    H = GC // 2
+    block(gather_v, 0, SPLIT, s.yv1)
+    block(gather_s, H, H + SPLIT, s.ys1)
+    block(gather_v, SPLIT, H, s.yv2)
+    block(gather_s, H + SPLIT, GC, s.ys2)
+    for a, b, sem in ((0, SPLIT, s.yv1), (H, H + SPLIT, s.ys1), (SPLIT, H, s.yv2)):
+        Y.wait_ge(sem, 1)
+        Y.dma_start(T.y[:, a:b], T.ys[:, a:b]).then_inc(s.st, 16)
+    S.wait_ge(s.ys2, 1)
+    S.dma_start(T.y[:, H + SPLIT:GC], T.ys[:, H + SPLIT:GC]).then_inc(s.st2, 16)
+    Y.wait_ge(s.st, 48)
+    S.wait_ge(s.st2, 16)

@@ -1,8 +1,8 @@
-from concourse.mybir import AluOpType as A, ActivationFunctionType as F, AxisListType
+from concourse.mybir import AluOpType as A, ActivationFunctionType as F
 
 CAP, TC, GC = 512, 2048, 2048
 HALF = CAP // 2
-SPLIT = 384
+SPLIT = 768
 
 SCRATCH = {
     "xs": ("sbuf", [128, TC], "float32"),
@@ -41,7 +41,7 @@ SCRATCH = {
     "psb": ("psum", [128, 512], "float32"),
 }
 SEMAPHORES = ["lsnd", "lx", "lplc", "lgh", "i1", "i2", "v", "bz", "rr", "pa", "sos", "gf", "gn", "oh", "pb", "offs",
-              "sent", "afar", "anear", "yv1", "ys1", "yv2", "ys2", "st", "st2"]
+              "sent", "afar", "anear", "y1", "y2", "st"]
 
 
 def rank_program(g, core, T, topo):
@@ -64,8 +64,12 @@ def rank_program(g, core, T, topo):
     def slot(dst):
         return GC + CAP if dst == lo else GC
 
-    far_mask = topo.mask(core, far)
-    near_mask = topo.mask(core, near) & ~far_mask
+    def every_other(mask):
+        bits = [e for e in range(mask.bit_length()) if mask >> e & 1]
+        return sum(1 << e for e in bits[::2])
+
+    far_mask = every_other(topo.mask(core, far))
+    near_mask = every_other(topo.mask(core, near) & ~topo.mask(core, far))
     n_far, n_near = bin(far_mask).count("1"), bin(near_mask).count("1")
 
     Y.dma_start(T.sndi[:], T.snd[:]).then_inc(s.lsnd, 16)
@@ -92,6 +96,14 @@ def rank_program(g, core, T, topo):
     V.memset(T.negz[:], -0.0).then_inc(s.bz, 1)
     V.wait_ge(s.i1, 1)
     V.tensor_scalar(T.rep[:], T.dq[:], 0.0, None, A.is_equal).then_inc(s.rr, 1)
+    V.wait_ge(s.lsnd, 16)
+    V.tensor_copy(T.sndf[:], T.sndi[:]).then_inc(s.rr, 1)
+
+    P.wait_ge(s.rr, 2)
+    P.matmul(T.psa[:, 0:64], T.rep[:], T.sndf[:], True, True).then_inc(s.pa, 1)
+
+    V.wait_ge(s.pa, 1)
+    V.tensor_copy(T.so[:], T.psa[:, 0:64]).then_inc(s.sos, 1)
     V.wait_ge(s.i2, 5)
     v(V.tensor_scalar(T.ip3[:], T.ip[:], 3, None, A.arith_shift_right))
     v(V.tensor_scalar(T.ip15[:], T.ip[:], 15, None, A.bitwise_and))
@@ -101,14 +113,7 @@ def rank_program(g, core, T, topo):
     vw()
     v(V.tensor_tensor(T.jw[:], T.jbase[:], T.jm[:], A.add))
     v(V.tensor_scalar(T.mm[:], T.io16[:], T.p15[:, 0:1], None, A.add))
-    V.wait_ge(s.lsnd, 16)
-    V.tensor_copy(T.sndf[:], T.sndi[:]).then_inc(s.rr, 1)
 
-    P.wait_ge(s.rr, 2)
-    P.matmul(T.psa[:, 0:64], T.rep[:], T.sndf[:], True, True).then_inc(s.pa, 1)
-
-    V.wait_ge(s.pa, 1)
-    V.tensor_copy(T.so[:], T.psa[:, 0:64]).then_inc(s.sos, 1)
     V.wait_ge(s.sos, 1)
     V.wait_ge(s.lx, 16)
     S.wait_ge(s.bz, 1)
@@ -162,19 +167,10 @@ def rank_program(g, core, T, topo):
         q.wait_ge(s.lgh, 16)
         q.wait_ge(s.anear, n_near)
         q.wait_ge(s.afar, n_far)
-
-    def block(f, a, b, sem):
-        f(T.ys[:, a:b], T.w[:], T.off[:, a // 16:b // 16], sem)
-
-    H = GC // 2
-    block(gather_v, 0, SPLIT, s.yv1)
-    block(gather_s, H, H + SPLIT, s.ys1)
-    block(gather_v, SPLIT, H, s.yv2)
-    block(gather_s, H + SPLIT, GC, s.ys2)
-    for a, b, sem in ((0, SPLIT, s.yv1), (H, H + SPLIT, s.ys1), (SPLIT, H, s.yv2)):
-        Y.wait_ge(sem, 1)
+    for a, b, sem in ((0, SPLIT, s.y1), (SPLIT, GC, s.y2)):
+        m = (a + b) // 2
+        gather_v(T.ys[:, a:m], T.w[:], T.off[:, a // 16:m // 16], sem)
+        gather_s(T.ys[:, m:b], T.w[:], T.off[:, m // 16:b // 16], sem)
+        Y.wait_ge(sem, 2)
         Y.dma_start(T.y[:, a:b], T.ys[:, a:b]).then_inc(s.st, 16)
-    S.wait_ge(s.ys2, 1)
-    S.dma_start(T.y[:, H + SPLIT:GC], T.ys[:, H + SPLIT:GC]).then_inc(s.st2, 16)
-    Y.wait_ge(s.st, 48)
-    S.wait_ge(s.st2, 16)
+    Y.wait_ge(s.st, 32)

@@ -1,14 +1,15 @@
 from concourse.mybir import AluOpType as A, ActivationFunctionType as F
 
 CAP, TC, GC = 512, 2048, 2048
-HALF = CAP // 2
-SPLIT = 768
+REL = 64
+SPLIT = 640
 
 SCRATCH = {
     "xs": ("sbuf", [128, TC], "float32"),
     "w": ("sbuf", [128, GC + 2 * CAP], "float32"),
     "ys": ("sbuf", [128, GC], "float32"),
     "sb": ("sbuf", [128, 2 * CAP], "float32"),
+    "rl": ("sbuf", [128, REL], "float32"),
     "negz": ("sbuf", [128, 4], "float32"),
     "sndi": ("sbuf", [16, 64], "int32"),
     "sndf": ("sbuf", [16, 64], "float32"),
@@ -40,8 +41,8 @@ SCRATCH = {
     "psa": ("psum", [128, 512], "float32"),
     "psb": ("psum", [128, 512], "float32"),
 }
-SEMAPHORES = ["lsnd", "lx", "lplc", "lgh", "i1", "i2", "v", "bz", "rr", "pa", "sos", "gf", "gn", "oh", "pb", "offs",
-              "sent", "afar", "anear", "y1", "y2", "st"]
+SEMAPHORES = ["lsnd", "lx", "lplc", "lgh", "i1", "i2", "v", "bz", "rr", "pa", "sos", "gf1", "gr", "gf2", "gn", "oh", "pb",
+              "offs", "sent", "afar", "arel", "anear", "y1", "y2", "st"]
 
 
 def rank_program(g, core, T, topo):
@@ -49,20 +50,26 @@ def rank_program(g, core, T, topo):
     if rank is None:
         return
     n = len(T.cores)
-    lo, hi = T.cores[(rank - 1) % n], T.cores[(rank + 1) % n]
+
+    def sides(c):
+        r = T.rank_of(c)
+        return T.cores[(r - 1) % n], T.cores[(r + 1) % n]
+
+    lo, hi = sides(core)
 
     def here(c):
         return topo.host(c) == topo.host(core) and topo.chip(c) == topo.chip(core)
 
     near, far = (lo, hi) if here(lo) else (hi, lo)
+    beyond = [c for c in sides(near) if c != core][0]
     s = T.sem
     V, S, P, Y = g.vector, g.scalar, g.tensor, g.sync
 
     def half(dst):
         return 0 if dst == lo else 1
 
-    def slot(dst):
-        return GC + CAP if dst == lo else GC
+    def slot(src, dst):
+        return GC + CAP if dst == sides(src)[0] else GC
 
     def every_other(mask):
         bits = [e for e in range(mask.bit_length()) if mask >> e & 1]
@@ -70,7 +77,8 @@ def rank_program(g, core, T, topo):
 
     far_mask = every_other(topo.mask(core, far))
     near_mask = every_other(topo.mask(core, near) & ~topo.mask(core, far))
-    n_far, n_near = bin(far_mask).count("1"), bin(near_mask).count("1")
+    fwd_mask = every_other(topo.mask(core, beyond))
+    n_far, n_near, n_fwd = [bin(m).count("1") for m in (far_mask, near_mask, fwd_mask)]
 
     Y.dma_start(T.sndi[:], T.snd[:]).then_inc(s.lsnd, 16)
     Y.dma_start(T.xs[:], T.x[:]).then_inc(s.lx, 16)
@@ -104,15 +112,6 @@ def rank_program(g, core, T, topo):
 
     V.wait_ge(s.pa, 1)
     V.tensor_copy(T.so[:], T.psa[:, 0:64]).then_inc(s.sos, 1)
-    V.wait_ge(s.i2, 5)
-    v(V.tensor_scalar(T.ip3[:], T.ip[:], 3, None, A.arith_shift_right))
-    v(V.tensor_scalar(T.ip15[:], T.ip[:], 15, None, A.bitwise_and))
-    vw()
-    v(V.tensor_scalar(T.jm[:], T.ip3[:], -1023.0, None, A.mult))
-    v(V.tensor_copy(T.p15[:], T.ip15[:]))
-    vw()
-    v(V.tensor_tensor(T.jw[:], T.jbase[:], T.jm[:], A.add))
-    v(V.tensor_scalar(T.mm[:], T.io16[:], T.p15[:, 0:1], None, A.add))
 
     V.wait_ge(s.sos, 1)
     V.wait_ge(s.lx, 16)
@@ -126,27 +125,54 @@ def rank_program(g, core, T, topo):
     def gather_s(out, win, off, sem):
         S.activation(out, win.indirect(off), F.Identity, bias=T.negz[:, 0:1]).then_inc(sem, 1)
 
-    for dst, base, sem in ((far, 0, s.gf), (near, CAP, s.gn)):
-        o = 32 * half(dst)
-        gather_v(T.sb[:, base:base + HALF], T.xs[:], T.so[:, o:o + 16], sem)
-        gather_s(T.sb[:, base + HALF:base + CAP], T.xs[:], T.so[:, o + 16:o + 32], sem)
+    def both(out, win, off, sem):
+        (ot, a, b), (ft, c) = out, off
+        m = (a + b) // 2
+        k = (m - a) // 16
+        gather_v(ot[:, a:m], win, ft[:, c:c + k], sem)
+        gather_s(ot[:, m:b], win, ft[:, c + k:c + 2 * k], sem)
 
-    for dst, base, sem, mask, arr in ((far, 0, s.gf, far_mask, s.afar), (near, CAP, s.gn, near_mask, s.anear)):
+    def send(dst, to, src, arr, mask):
         rid, pid = topo.addr(dst, core)
-        g.wait_ge(sem, 2)
-        g.remote_dma(T.w[:, slot(dst):slot(dst) + CAP], T.sb[:, base:base + CAP], arr, s.sent, pid, rid, mask)
-    g.wait_ge(s.sent, n_far + n_near)
+        g.remote_dma(to, src, arr, s.sent, pid, rid, mask)
 
+    MID = CAP // 2
+    for dst, a, b, base, sem in ((far, REL, MID, 0, s.gf1), (far, 0, REL, 0, s.gr), (far, MID, CAP, 0, s.gf2),
+                                 (near, 0, CAP, CAP, s.gn)):
+        both((T.sb, base + a, base + b), T.xs[:], (T.so, 32 * half(dst) + a // 16), sem)
+        g.wait_ge(sem, 2)
+        piece, c = T.sb[:, base + a:base + b], slot(core, dst)
+        if dst == far and a == 0:
+            send(near, T.rl[:], piece, s.arel, near_mask)
+        elif dst == far:
+            send(far, T.w[:, c + a:c + b], piece, s.afar, far_mask)
+        else:
+            send(near, T.w[:, c + a:c + b], piece, s.anear, near_mask)
+    g.wait_ge(s.arel, n_near)
+    c = slot(near, beyond)
+    send(beyond, T.w[:, c:c + REL], T.rl[:], s.afar, fwd_mask)
+    g.wait_ge(s.sent, 2 * n_far + 2 * n_near + n_fwd)
+
+    V.wait_ge(s.i2, 5)
     V.wait_ge(s.lplc, 16)
+    v(V.tensor_scalar(T.ip3[:], T.ip[:], 3, None, A.arith_shift_right))
+    v(V.tensor_scalar(T.ip15[:], T.ip[:], 15, None, A.bitwise_and))
     v(V.tensor_scalar(T.kki[:], T.pli[:], 4, None, A.arith_shift_right))
     v(V.tensor_scalar(T.qqi[:], T.pli[:], 15, None, A.bitwise_and))
     vw()
+    v(V.tensor_scalar(T.jm[:], T.ip3[:], -1023.0, None, A.mult))
+    v(V.tensor_copy(T.p15[:], T.ip15[:]))
     v(V.tensor_copy(T.kkf[:], T.kki[:]))
     v(V.tensor_copy(T.qqf[:], T.qqi[:]))
     vw()
+    v(V.tensor_tensor(T.jw[:], T.jbase[:], T.jm[:], A.add))
+    v(V.tensor_scalar(T.mm[:], T.io16[:], T.p15[:, 0:1], None, A.add))
     for c in range(8):
         b = slice(128 * c, 128 * c + 128)
         V.tensor_scalar(T.ohq[:, b], T.ioq[:], T.qqf[:, c:c + 1], None, A.is_equal).then_inc(s.oh, 1)
+    vw()
+    for c in range(8):
+        b = slice(128 * c, 128 * c + 128)
         V.tensor_scalar(T.ohk[:, b], T.iok[:], T.kkf[:, c:c + 1], T.jw[:, c:c + 1], A.is_equal, A.mult).then_inc(s.oh, 1)
     P.wait_ge(s.oh, 16)
     for c in range(8):
@@ -166,11 +192,9 @@ def rank_program(g, core, T, topo):
         q.wait_ge(s.offs, 1)
         q.wait_ge(s.lgh, 16)
         q.wait_ge(s.anear, n_near)
-        q.wait_ge(s.afar, n_far)
+        q.wait_ge(s.afar, 2 * n_far + n_fwd)
     for a, b, sem in ((0, SPLIT, s.y1), (SPLIT, GC, s.y2)):
-        m = (a + b) // 2
-        gather_v(T.ys[:, a:m], T.w[:], T.off[:, a // 16:m // 16], sem)
-        gather_s(T.ys[:, m:b], T.w[:], T.off[:, m // 16:b // 16], sem)
+        both((T.ys, a, b), T.w[:], (T.off, a // 16), sem)
         Y.wait_ge(sem, 2)
         Y.dma_start(T.y[:, a:b], T.ys[:, a:b]).then_inc(s.st, 16)
     Y.wait_ge(s.st, 32)

@@ -1,7 +1,7 @@
 from concourse.mybir import AluOpType as A, ActivationFunctionType as F
 
 CAP, TC, GC = 512, 2048, 2048
-REL = 64
+REL = 128
 SPLIT = 640
 
 SCRATCH = {

@@ -1,7 +1,12 @@
+from concourse.bass import DstId, RemoteDMATransfer
 from concourse.mybir import AluOpType as A, ActivationFunctionType as F
 
 CAP, TC, GC = 512, 2048, 2048
-REL = 128
+WORLD = 512
+CABLE, SWITCH = (64, 64, 144), (128, 0, 160)
+REL = max(CABLE + SWITCH)
+REL_N = 4
+CUT = (0, 128, 320, CAP)
 SPLIT = 640
 
 SCRATCH = {
@@ -41,44 +46,87 @@ SCRATCH = {
     "psa": ("psum", [128, 512], "float32"),
     "psb": ("psum", [128, 512], "float32"),
 }
-SEMAPHORES = ["lsnd", "lx", "lplc", "lgh", "i1", "i2", "v", "bz", "rr", "pa", "sos", "gf1", "gr", "gf2", "gn", "oh", "pb",
+SEMAPHORES = ["lsnd", "lx", "lplc", "lgh", "i1", "i2", "v", "bz", "rr", "pa", "sos", "gf1", "gf2", "gf3", "gn", "oh", "pb",
               "offs", "sent", "afar", "arel", "anear", "y1", "y2", "st"]
 
 
 def rank_program(g, core, T, topo):
-    rank = T.rank_of(core)
-    if rank is None:
-        return
     n = len(T.cores)
+    s = T.sem
+
+    def same_chip(a, b):
+        return topo.host(a) == topo.host(b) and topo.chip(a) == topo.chip(b)
+
+    if not any(same_chip(core, c) for c in T.cores):
+        return
 
     def sides(c):
         r = T.rank_of(c)
         return T.cores[(r - 1) % n], T.cores[(r + 1) % n]
 
+    def near_of(c):
+        return [d for d in sides(c) if same_chip(c, d)][0]
+
+    def far_of(c):
+        return [d for d in sides(c) if not same_chip(c, d)][0]
+
+    def plan(c):
+        return SWITCH if topo.same_plane(c, far_of(c)) else CABLE
+
+    def owns_port(c):
+        return any(topo.mates(c, m) and topo.may_write(c, m) for m in range(WORLD))
+
+    def helper_of(c):
+        return [h for h in range(WORLD) if h != c and same_chip(h, c) and topo.die(h) == topo.die(c) and owns_port(h)][0]
+
+    def slot(src, dst):
+        return GC + CAP if dst == sides(src)[0] else GC
+
+    def bits(mask):
+        return [e for e in range(mask.bit_length()) if mask >> e & 1]
+
+    def engines(es):
+        return sum(1 << e for e in es)
+
+    def addr(dst):
+        rid, pid = topo.addr(dst, core)
+        return DstId(rid=rid, pnc=pid)
+
+    def off_mask(dst):
+        return engines(bits(topo.mask(core, dst))[::2])
+
+    sent = [0]
+
+    def send(*ts):
+        g.remote_dma_fused([RemoteDMATransfer(dst_ids=[addr(dst)], dma_engine_mask=m, remote_sem=sem, src=src, dst=to)
+                            for dst, to, src, sem, m in ts], local_sem=s.sent)
+        sent[0] += sum(len(bits(t[4])) for t in ts)
+
+    def pass_on(c, a, b):
+        g.wait_ge(s.arel, REL_N)
+        to, at = far_of(c), slot(c, far_of(c))
+        send((to, T.w[:, at + a:at + b], T.rl[:, 0:b - a], s.afar, off_mask(to)))
+        g.wait_ge(s.sent, sent[0])
+
+    if T.rank_of(core) is None:
+        for c in T.cores:
+            first, hel, nea = plan(c)
+            if hel and same_chip(core, c) and core == helper_of(c):
+                pass_on(c, first, first + hel)
+        return
+
     lo, hi = sides(core)
-
-    def here(c):
-        return topo.host(c) == topo.host(core) and topo.chip(c) == topo.chip(core)
-
-    near, far = (lo, hi) if here(lo) else (hi, lo)
-    beyond = [c for c in sides(near) if c != core][0]
-    s = T.sem
+    near, far = near_of(core), far_of(core)
     V, S, P, Y = g.vector, g.scalar, g.tensor, g.sync
 
     def half(dst):
         return 0 if dst == lo else 1
 
-    def slot(src, dst):
-        return GC + CAP if dst == sides(src)[0] else GC
-
-    def every_other(mask):
-        bits = [e for e in range(mask.bit_length()) if mask >> e & 1]
-        return sum(1 << e for e in bits[::2])
-
-    far_mask = every_other(topo.mask(core, far))
-    near_mask = every_other(topo.mask(core, near) & ~topo.mask(core, far))
-    fwd_mask = every_other(topo.mask(core, beyond))
-    n_far, n_near, n_fwd = [bin(m).count("1") for m in (far_mask, near_mask, fwd_mask)]
+    inner = bits(topo.mask(core, near) & ~topo.mask(core, far))
+    far_mask, hel_mask, rel_mask = off_mask(far), engines(inner[::2]), engines(inner[1::2])
+    near_mask = engines(inner)
+    n_near = len(inner)
+    n_far = len(bits(far_mask)) * (4 if plan(far)[1] else 3)
 
     Y.dma_start(T.sndi[:], T.snd[:]).then_inc(s.lsnd, 16)
     Y.dma_start(T.xs[:], T.x[:]).then_inc(s.lx, 16)
@@ -132,26 +180,31 @@ def rank_program(g, core, T, topo):
         gather_v(ot[:, a:m], win, ft[:, c:c + k], sem)
         gather_s(ot[:, m:b], win, ft[:, c + k:c + 2 * k], sem)
 
-    def send(dst, to, src, arr, mask):
-        rid, pid = topo.addr(dst, core)
-        g.remote_dma(to, src, arr, s.sent, pid, rid, mask)
+    for i, sem in enumerate((s.gf1, s.gf2, s.gf3)):
+        a, b = CUT[i], CUT[i + 1]
+        both((T.sb, a, b), T.xs[:], (T.so, 32 * half(far) + a // 16), sem)
+    both((T.sb, CAP, 2 * CAP), T.xs[:], (T.so, 32 * half(near)), s.gn)
 
-    MID = CAP // 2
-    for dst, a, b, base, sem in ((far, REL, MID, 0, s.gf1), (far, 0, REL, 0, s.gr), (far, MID, CAP, 0, s.gf2),
-                                 (near, 0, CAP, CAP, s.gn)):
-        both((T.sb, base + a, base + b), T.xs[:], (T.so, 32 * half(dst) + a // 16), sem)
-        g.wait_ge(sem, 2)
-        piece, c = T.sb[:, base + a:base + b], slot(core, dst)
-        if dst == far and a == 0:
-            send(near, T.rl[:], piece, s.arel, near_mask)
-        elif dst == far:
-            send(far, T.w[:, c + a:c + b], piece, s.afar, far_mask)
-        else:
-            send(near, T.w[:, c + a:c + b], piece, s.anear, near_mask)
-    g.wait_ge(s.arel, n_near)
-    c = slot(near, beyond)
-    send(beyond, T.w[:, c:c + REL], T.rl[:], s.afar, fwd_mask)
-    g.wait_ge(s.sent, 2 * n_far + 2 * n_near + n_fwd)
+    first, hel, nea = plan(core)
+    p, q = first + hel, first + hel + nea
+    fs, ns = slot(core, far), slot(core, near)
+
+    def direct(a, b):
+        return far, T.w[:, fs + a:fs + b], T.sb[:, a:b], s.afar, far_mask
+
+    g.wait_ge(s.gf1, 2)
+    if hel:
+        send(direct(0, first), (helper_of(core), T.rl[:, 0:hel], T.sb[:, first:p], s.arel, hel_mask))
+    else:
+        send(direct(0, first))
+    g.wait_ge(s.gf2, 2)
+    send((near, T.rl[:, 0:nea], T.sb[:, p:q], s.arel, rel_mask))
+    g.wait_ge(s.gf3, 2)
+    send(direct(q, CAP))
+    g.wait_ge(s.gn, 2)
+    send((near, T.w[:, ns:ns + CAP], T.sb[:, CAP:2 * CAP], s.anear, near_mask))
+    first, hel, nea = plan(near)
+    pass_on(near, first + hel, first + hel + nea)
 
     V.wait_ge(s.i2, 5)
     V.wait_ge(s.lplc, 16)
@@ -188,11 +241,11 @@ def rank_program(g, core, T, topo):
     vw()
     V.tensor_copy(T.off[:], T.t3[:]).then_inc(s.offs, 1)
 
-    for q in (V, S):
-        q.wait_ge(s.offs, 1)
-        q.wait_ge(s.lgh, 16)
-        q.wait_ge(s.anear, n_near)
-        q.wait_ge(s.afar, 2 * n_far + n_fwd)
+    for e in (V, S):
+        e.wait_ge(s.offs, 1)
+        e.wait_ge(s.lgh, 16)
+        e.wait_ge(s.anear, n_near)
+        e.wait_ge(s.afar, n_far)
     for a, b, sem in ((0, SPLIT, s.y1), (SPLIT, GC, s.y2)):
         both((T.ys, a, b), T.w[:], (T.off, a // 16), sem)
         Y.wait_ge(sem, 2)

@@ -3,10 +3,9 @@ from concourse.mybir import AluOpType as A, ActivationFunctionType as F
 
 CAP, TC, GC = 512, 2048, 2048
 WORLD = 512
-CABLE, SWITCH = (64, 64, 144), (128, 0, 160)
+CABLE, SWITCH = (64, 64, 2, 144), (192, 0, 0, 160)
 REL = max(CABLE + SWITCH)
-REL_N = 4
-CUT = (0, 128, 320, CAP)
+CUT = (0, 192, 384, CAP)
 SPLIT = 640
 
 SCRATCH = {
@@ -76,8 +75,11 @@ def rank_program(g, core, T, topo):
     def owns_port(c):
         return any(topo.mates(c, m) and topo.may_write(c, m) for m in range(WORLD))
 
-    def helper_of(c):
-        return [h for h in range(WORLD) if h != c and same_chip(h, c) and topo.die(h) == topo.die(c) and owns_port(h)][0]
+    def helpers_of(c):
+        own = [h for h in range(WORLD) if same_chip(h, c) and owns_port(h)]
+        same = [h for h in own if topo.die(h) == topo.die(c)]
+        other = [h for h in own if topo.die(h) != topo.die(c)]
+        return [same[0], other[0]][:plan(c)[2]]
 
     def slot(src, dst):
         return GC + CAP if dst == sides(src)[0] else GC
@@ -95,6 +97,9 @@ def rank_program(g, core, T, topo):
     def off_mask(dst):
         return engines(bits(topo.mask(core, dst))[::2])
 
+    def inner(c):
+        return bits(topo.mask(c, near_of(c)) & ~topo.mask(c, far_of(c)))
+
     sent = [0]
 
     def send(*ts):
@@ -102,17 +107,18 @@ def rank_program(g, core, T, topo):
                             for dst, to, src, sem, m in ts], local_sem=s.sent)
         sent[0] += sum(len(bits(t[4])) for t in ts)
 
-    def pass_on(c, a, b):
-        g.wait_ge(s.arel, REL_N)
+    def pass_on(c, a, b, n_in):
+        g.wait_ge(s.arel, n_in)
         to, at = far_of(c), slot(c, far_of(c))
         send((to, T.w[:, at + a:at + b], T.rl[:, 0:b - a], s.afar, off_mask(to)))
         g.wait_ge(s.sent, sent[0])
 
     if T.rank_of(core) is None:
         for c in T.cores:
-            first, hel, nea = plan(c)
-            if hel and same_chip(core, c) and core == helper_of(c):
-                pass_on(c, first, first + hel)
+            first, hel, nh, nea = plan(c)
+            if nh and same_chip(core, c) and core in helpers_of(c):
+                i = helpers_of(c).index(core)
+                pass_on(c, first + i * hel, first + (i + 1) * hel, len(inner(c)[i::2]))
         return
 
     lo, hi = sides(core)
@@ -122,11 +128,9 @@ def rank_program(g, core, T, topo):
     def half(dst):
         return 0 if dst == lo else 1
 
-    inner = bits(topo.mask(core, near) & ~topo.mask(core, far))
-    far_mask, hel_mask, rel_mask = off_mask(far), engines(inner[::2]), engines(inner[1::2])
-    near_mask = engines(inner)
-    n_near = len(inner)
-    n_far = len(bits(far_mask)) * (4 if plan(far)[1] else 3)
+    far_mask, near_mask = off_mask(far), engines(inner(core))
+    n_near = len(inner(near))
+    n_far = len(bits(far_mask)) * (3 + plan(far)[2])
 
     Y.dma_start(T.sndi[:], T.snd[:]).then_inc(s.lsnd, 16)
     Y.dma_start(T.xs[:], T.x[:]).then_inc(s.lx, 16)
@@ -185,26 +189,29 @@ def rank_program(g, core, T, topo):
         both((T.sb, a, b), T.xs[:], (T.so, 32 * half(far) + a // 16), sem)
     both((T.sb, CAP, 2 * CAP), T.xs[:], (T.so, 32 * half(near)), s.gn)
 
-    first, hel, nea = plan(core)
-    p, q = first + hel, first + hel + nea
+    first, hel, nh, nea = plan(core)
+    p = first + nh * hel
+    q = p + nea
     fs, ns = slot(core, far), slot(core, near)
 
     def direct(a, b):
         return far, T.w[:, fs + a:fs + b], T.sb[:, a:b], s.afar, far_mask
 
+    def share(i):
+        h, a = helpers_of(core)[i], first + i * hel
+        return h, T.rl[:, 0:hel], T.sb[:, a:a + hel], s.arel, engines(inner(core)[i::2])
+
     g.wait_ge(s.gf1, 2)
-    if hel:
-        send(direct(0, first), (helper_of(core), T.rl[:, 0:hel], T.sb[:, first:p], s.arel, hel_mask))
-    else:
-        send(direct(0, first))
+    send(direct(0, first), *[share(i) for i in range(nh)])
     g.wait_ge(s.gf2, 2)
-    send((near, T.rl[:, 0:nea], T.sb[:, p:q], s.arel, rel_mask))
+    send((near, T.rl[:, 0:nea], T.sb[:, p:q], s.arel, near_mask))
     g.wait_ge(s.gf3, 2)
     send(direct(q, CAP))
     g.wait_ge(s.gn, 2)
     send((near, T.w[:, ns:ns + CAP], T.sb[:, CAP:2 * CAP], s.anear, near_mask))
-    first, hel, nea = plan(near)
-    pass_on(near, first + hel, first + hel + nea)
+    first, hel, nh, nea = plan(near)
+    p = first + nh * hel
+    pass_on(near, p, p + nea, n_near)
 
     V.wait_ge(s.i2, 5)
     V.wait_ge(s.lplc, 16)

@@ -2,10 +2,11 @@ from concourse.bass import DstId, RemoteDMATransfer
 from concourse.mybir import AluOpType as A, ActivationFunctionType as F
 
 CAP, TC, GC = 512, 2048, 2048
+H = GC // 2
 WORLD = 512
-CABLE, SWITCH = (64, 64, 2, 144), (192, 0, 0, 160)
-REL = max(CABLE + SWITCH)
-CUT = (0, 192, 384, CAP)
+CABLE, SWITCH = (104, 2), (176, 0)
+PARTS = {CABLE: ((224, 192), (64, 32)), SWITCH: ((192, 160), (96, 64))}
+NEAR_V = 224
 SPLIT = 640
 
 SCRATCH = {
@@ -13,50 +14,57 @@ SCRATCH = {
     "w": ("sbuf", [128, GC + 2 * CAP], "float32"),
     "ys": ("sbuf", [128, GC], "float32"),
     "sb": ("sbuf", [128, 2 * CAP], "float32"),
-    "rl": ("sbuf", [128, REL], "float32"),
+    "rl": ("sbuf", [128, max(CABLE[0], SWITCH[0])], "float32"),
     "negz": ("sbuf", [128, 4], "float32"),
-    "sndi": ("sbuf", [16, 64], "int32"),
-    "sndf": ("sbuf", [16, 64], "float32"),
+    "li": ("sbuf", [16, 128], "int32"),
+    "lf": ("sbuf", [16, 128], "float32"),
     "dq": ("sbuf", [16, 128], "float32"),
     "rep": ("sbuf", [16, 128], "float32"),
     "so": ("sbuf", [128, 64], "uint16"),
-    "pli": ("sbuf", [128, 8], "int32"),
+    "spr": ("sbuf", [128, 64], "float32"),
+    "pick": ("sbuf", [128, 2], "uint16"),
+    "pl": ("sbuf", [128, 16], "int32"),
     "kki": ("sbuf", [128, 8], "int32"),
     "qqi": ("sbuf", [128, 8], "int32"),
     "kkf": ("sbuf", [128, 8], "float32"),
     "qqf": ("sbuf", [128, 8], "float32"),
-    "ip": ("sbuf", [128, 8], "int32"),
-    "ip3": ("sbuf", [128, 8], "int32"),
-    "ip15": ("sbuf", [128, 8], "int32"),
-    "p15": ("sbuf", [128, 8], "float32"),
-    "jbase": ("sbuf", [128, 8], "float32"),
-    "jm": ("sbuf", [128, 8], "float32"),
+    "neg": ("sbuf", [128, 8], "float32"),
+    "big": ("sbuf", [128, 8], "float32"),
+    "nb": ("sbuf", [128, 8], "float32"),
+    "ja": ("sbuf", [128, 8], "float32"),
+    "jb": ("sbuf", [128, 8], "float32"),
     "jw": ("sbuf", [128, 8], "float32"),
+    "ip": ("sbuf", [128, 4], "int32"),
+    "ip4": ("sbuf", [128, 4], "int32"),
+    "ipm": ("sbuf", [128, 4], "int32"),
+    "jm": ("sbuf", [128, 4], "float32"),
+    "g8": ("sbuf", [128, 4], "float32"),
+    "pmf": ("sbuf", [128, 4], "float32"),
     "iok": ("sbuf", [128, 128], "bfloat16"),
     "ioq": ("sbuf", [128, 128], "bfloat16"),
     "io16": ("sbuf", [128, 128], "float32"),
-    "mm": ("sbuf", [128, 128], "float32"),
+    "base": ("sbuf", [128, 128], "float32"),
     "ohq": ("sbuf", [128, 1024], "float16"),
     "ohk": ("sbuf", [128, 1024], "float16"),
-    "t1": ("sbuf", [128, 128], "float32"),
-    "t2": ("sbuf", [128, 128], "float32"),
-    "t3": ("sbuf", [128, 128], "float32"),
+    "offf": ("sbuf", [128, 128], "float32"),
     "off": ("sbuf", [128, 128], "uint16"),
     "psa": ("psum", [128, 512], "float32"),
     "psb": ("psum", [128, 512], "float32"),
 }
-SEMAPHORES = ["lsnd", "lx", "lplc", "lgh", "i1", "i2", "v", "bz", "rr", "pa", "sos", "gf1", "gf2", "gf3", "gn", "oh", "pb",
-              "offs", "sent", "afar", "arel", "anear", "y1", "y2", "st"]
+SEMAPHORES = ["lsnd", "lx", "lplc", "lgh", "i1", "i2", "ik", "v", "bz", "rr", "pa", "sos", "gf1", "gf2", "gn", "oh", "pb",
+              "made", "offs", "sent", "tab", "afar", "arel", "anear", "y1", "y2", "st"]
 
 
 def rank_program(g, core, T, topo):
     n = len(T.cores)
     s = T.sem
+    V, S, P, Y = g.vector, g.scalar, g.tensor, g.sync
 
     def same_chip(a, b):
         return topo.host(a) == topo.host(b) and topo.chip(a) == topo.chip(b)
 
-    if not any(same_chip(core, c) for c in T.cores):
+    ranks = [c for c in T.cores if same_chip(core, c)]
+    if not ranks:
         return
 
     def sides(c):
@@ -75,14 +83,12 @@ def rank_program(g, core, T, topo):
     def owns_port(c):
         return any(topo.mates(c, m) and topo.may_write(c, m) for m in range(WORLD))
 
-    def helpers_of(c):
-        own = [h for h in range(WORLD) if same_chip(h, c) and owns_port(h)]
-        same = [h for h in own if topo.die(h) == topo.die(c)]
-        other = [h for h in own if topo.die(h) != topo.die(c)]
-        return [same[0], other[0]][:plan(c)[2]]
+    relayed = [c for c in ranks if plan(c)[1]][0]
+    own = [h for h in range(WORLD) if same_chip(h, core) and T.rank_of(h) is None and owns_port(h)]
+    helpers = [[h for h in own if topo.die(h) == topo.die(relayed)][0], [h for h in own if topo.die(h) != topo.die(relayed)][0]]
 
     def slot(src, dst):
-        return GC + CAP if dst == sides(src)[0] else GC
+        return H + CAP if dst == sides(src)[0] else H
 
     def bits(mask):
         return [e for e in range(mask.bit_length()) if mask >> e & 1]
@@ -94,55 +100,27 @@ def rank_program(g, core, T, topo):
         rid, pid = topo.addr(dst, core)
         return DstId(rid=rid, pnc=pid)
 
-    def off_mask(dst):
-        return engines(bits(topo.mask(core, dst))[::2])
+    def outer(c):
+        return bits(topo.mask(c, far_of(c)))
 
     def inner(c):
         return bits(topo.mask(c, near_of(c)) & ~topo.mask(c, far_of(c)))
 
+    def near_share(c):
+        return outer(c)[1::2] if plan(c)[1] else inner(c)
+
     sent = [0]
 
     def send(*ts):
-        g.remote_dma_fused([RemoteDMATransfer(dst_ids=[addr(dst)], dma_engine_mask=m, remote_sem=sem, src=src, dst=to)
-                            for dst, to, src, sem, m in ts], local_sem=s.sent)
-        sent[0] += sum(len(bits(t[4])) for t in ts)
+        g.remote_dma_fused([RemoteDMATransfer(dst_ids=[addr(d) for d in dsts], dma_engine_mask=engines(es), remote_sem=sem,
+                                              srcs=[src], dsts=[to for d in dsts])
+                            for dsts, to, src, sem, es in ts], local_sem=s.sent)
+        sent[0] += sum(len(t[4]) for t in ts)
 
     def pass_on(c, a, b, n_in):
         g.wait_ge(s.arel, n_in)
         to, at = far_of(c), slot(c, far_of(c))
-        send((to, T.w[:, at + a:at + b], T.rl[:, 0:b - a], s.afar, off_mask(to)))
-        g.wait_ge(s.sent, sent[0])
-
-    if T.rank_of(core) is None:
-        for c in T.cores:
-            first, hel, nh, nea = plan(c)
-            if nh and same_chip(core, c) and core in helpers_of(c):
-                i = helpers_of(c).index(core)
-                pass_on(c, first + i * hel, first + (i + 1) * hel, len(inner(c)[i::2]))
-        return
-
-    lo, hi = sides(core)
-    near, far = near_of(core), far_of(core)
-    V, S, P, Y = g.vector, g.scalar, g.tensor, g.sync
-
-    def half(dst):
-        return 0 if dst == lo else 1
-
-    far_mask, near_mask = off_mask(far), engines(inner(core))
-    n_near = len(inner(near))
-    n_far = len(bits(far_mask)) * (3 + plan(far)[2])
-
-    Y.dma_start(T.sndi[:], T.snd[:]).then_inc(s.lsnd, 16)
-    Y.dma_start(T.xs[:], T.x[:]).then_inc(s.lx, 16)
-    Y.dma_start(T.pli[:], T.plc[:]).then_inc(s.lplc, 16)
-    Y.dma_start(T.w[:, 0:GC], T.gh[:]).then_inc(s.lgh, 16)
-
-    g.iota(T.dq[:], [[0, 8], [1, 16]], 0, -1, allow_small_or_imprecise_dtypes=True).then_inc(s.i1, 1)
-    g.iota(T.ip[:], [[0, 8]], 0, 1).then_inc(s.i2, 1)
-    g.iota(T.jbase[:], [[16, 8]], 1, 128, allow_small_or_imprecise_dtypes=True).then_inc(s.i2, 1)
-    g.iota(T.io16[:], [[16, 128]], 0, 0, allow_small_or_imprecise_dtypes=True).then_inc(s.i2, 1)
-    g.iota(T.iok[:], [[1, 128]], 0, 0, allow_small_or_imprecise_dtypes=True).then_inc(s.i2, 1)
-    g.iota(T.ioq[:], [[0, 8], [1, 16]], 0, 0, allow_small_or_imprecise_dtypes=True).then_inc(s.i2, 1)
+        send(([to], T.w[:, at + a:at + b], T.rl[:, 0:b - a], s.afar, bits(topo.mask(core, to))))
 
     nv = [0]
 
@@ -153,17 +131,89 @@ def rank_program(g, core, T, topo):
     def vw():
         V.wait_ge(s.v, nv[0])
 
+    if T.rank_of(core) is None:
+        if core not in helpers:
+            return
+        i = helpers.index(core)
+        if i == 0:
+            g.iota(T.ip[:, 0:1], [[0, 1]], 0, 1).then_inc(s.i2, 1)
+            g.iota(T.io16[:], [[2 * H, 2], [16, 64]], 0, 0, allow_small_or_imprecise_dtypes=True).then_inc(s.i2, 1)
+            V.wait_ge(s.i2, 2)
+            v(V.tensor_scalar(T.ipm[:, 0:1], T.ip[:, 0:1], 15, None, A.bitwise_and))
+            vw()
+            v(V.tensor_copy(T.pmf[:, 0:1], T.ipm[:, 0:1]))
+            vw()
+            V.tensor_scalar(T.base[:], T.io16[:], T.pmf[:, 0:1], None, A.add).then_inc(s.made, 1)
+            table = T.base
+        else:
+            g.iota(T.ioq[:], [[0, 8], [1, 16]], 0, 0, allow_small_or_imprecise_dtypes=True).then_inc(s.made, 1)
+            table = T.ioq
+        g.wait_ge(s.made, 1)
+        send((ranks, table[:], table[:], s.tab, outer(relayed)))
+        wid = plan(relayed)[0]
+        pass_on(relayed, (1 + i) * wid, (2 + i) * wid, len(inner(relayed)[i::2]))
+        g.wait_ge(s.sent, sent[0])
+        return
+
+    lo, hi = sides(core)
+    near, far = near_of(core), far_of(core)
+    wid, nh = plan(core)
+
+    def half(dst):
+        return 0 if dst == lo else 1
+
+    every = bits(topo.mask(core, near))
+    direct_1 = outer(core)[::2] if nh else outer(core)
+    direct_2 = outer(core)
+    n_near = len(inner(near))
+    n_far = len(direct_1) + len(direct_2) + (1 + nh) * len(outer(core))
+    n_tab = len(every) + len(helpers) * len(outer(relayed))
+
+    S.dma_start(T.li[:, 64:128], T.plc[:]).then_inc(s.lplc, 16)
+    Y.dma_start(T.li[:, 0:64], T.snd[:]).then_inc(s.lsnd, 16)
+    Y.dma_start(T.xs[:], T.x[:]).then_inc(s.lx, 16)
+    Y.dma_start(T.w[:, 0:H], T.gh[:, 0:H]).then_inc(s.lgh, 16)
+    Y.dma_start(T.w[:, H + 2 * CAP:GC + 2 * CAP], T.gh[:, H:GC]).then_inc(s.lgh, 16)
+
+    mine = slice(64 * ranks.index(core), 64 * ranks.index(core) + 64)
+    g.iota(T.dq[:], [[0, 8], [1, 16]], 0, -1, allow_small_or_imprecise_dtypes=True).then_inc(s.i1, 1)
+    g.iota(T.iok[:, mine], [[1, 64]], 64 * ranks.index(core), 0, allow_small_or_imprecise_dtypes=True).then_inc(s.ik, 1)
+    g.iota(T.ja[:], [[16, 8]], H, 1, allow_small_or_imprecise_dtypes=True).then_inc(s.i2, 1)
+    g.wait_ge(s.ik, 1)
+    send(([near], T.iok[:, mine], T.iok[:, mine], s.tab, every))
+
     V.memset(T.negz[:], -0.0).then_inc(s.bz, 1)
     V.wait_ge(s.i1, 1)
     V.tensor_scalar(T.rep[:], T.dq[:], 0.0, None, A.is_equal).then_inc(s.rr, 1)
+    V.wait_ge(s.i2, 1)
+    v(V.tensor_scalar(T.ip[:, 0:1], T.ja[:, 0:1], -float(H), None, A.add))
     V.wait_ge(s.lsnd, 16)
-    V.tensor_copy(T.sndf[:], T.sndi[:]).then_inc(s.rr, 1)
+    V.wait_ge(s.lplc, 16)
+    V.tensor_copy(T.lf[:], T.li[:]).then_inc(s.rr, 1)
 
     P.wait_ge(s.rr, 2)
-    P.matmul(T.psa[:, 0:64], T.rep[:], T.sndf[:], True, True).then_inc(s.pa, 1)
+    P.matmul(T.psa[:, 0:128], T.rep[:], T.lf[:], True, True).then_inc(s.pa, 1)
 
+    vw()
+    v(V.tensor_scalar(T.ip4[:, 0:1], T.ip[:, 0:1], 4, None, A.arith_shift_right))
+    v(V.tensor_scalar(T.ipm[:, 0:1], T.ip[:, 0:1], 7, None, A.bitwise_and))
+    vw()
+    v(V.tensor_scalar(T.jm[:, 0:1], T.ip4[:, 0:1], 112.0, None, A.mult))
+    v(V.tensor_scalar(T.g8[:, 0:1], T.ip4[:, 0:1], 8.0, None, A.mult))
+    v(V.tensor_copy(T.pmf[:, 0:1], T.ipm[:, 0:1]))
     V.wait_ge(s.pa, 1)
     V.tensor_copy(T.so[:], T.psa[:, 0:64]).then_inc(s.sos, 1)
+    v(V.tensor_copy(T.spr[:], T.psa[:, 64:128]))
+    vw()
+    v(V.tensor_scalar(T.pick[:, 0:1], T.g8[:, 0:1], T.pmf[:, 0:1], None, A.add))
+    v(V.tensor_scalar(T.jb[:], T.ja[:], T.jm[:, 0:1], None, A.add))
+    vw()
+    v(V.tensor_copy(T.pl[:], T.spr[:].indirect(T.pick[:, 0:1])))
+    vw()
+    v(V.tensor_scalar(T.kki[:], T.pl[:, 0:8], 4, None, A.arith_shift_right))
+    v(V.tensor_scalar(T.qqi[:], T.pl[:, 0:8], 15, None, A.bitwise_and))
+    v(V.tensor_scalar(T.neg[:], T.pl[:, 0:8], -1.0, None, A.mult))
+    v(V.tensor_scalar(T.big[:], T.pl[:, 0:8], float(H), -float(H), A.is_ge, A.mult))
 
     V.wait_ge(s.sos, 1)
     V.wait_ge(s.lx, 16)
@@ -171,62 +221,42 @@ def rank_program(g, core, T, topo):
     S.wait_ge(s.sos, 1)
     S.wait_ge(s.lx, 16)
 
-    def gather_v(out, win, off, sem):
-        V.tensor_copy(out, win.indirect(off)).then_inc(sem, 1)
+    def both(out, a, nv_, ns_, win, off, c, sem):
+        k = nv_ // 16
+        V.tensor_copy(out[:, a:a + nv_], win.indirect(off[:, c:c + k])).then_inc(sem, 1)
+        S.activation(out[:, a + nv_:a + nv_ + ns_], win.indirect(off[:, c + k:c + k + ns_ // 16]), F.Identity,
+                     bias=T.negz[:, 0:1]).then_inc(sem, 1)
 
-    def gather_s(out, win, off, sem):
-        S.activation(out, win.indirect(off), F.Identity, bias=T.negz[:, 0:1]).then_inc(sem, 1)
+    a = 0
+    for (pv, ps), sem in zip(PARTS[plan(core)], (s.gf1, s.gf2)):
+        both(T.sb, a, pv, ps, T.xs[:], T.so, 32 * half(far) + a // 16, sem)
+        a += pv + ps
+    both(T.sb, CAP, NEAR_V, CAP - NEAR_V, T.xs[:], T.so, 32 * half(near), s.gn)
 
-    def both(out, win, off, sem):
-        (ot, a, b), (ft, c) = out, off
-        m = (a + b) // 2
-        k = (m - a) // 16
-        gather_v(ot[:, a:m], win, ft[:, c:c + k], sem)
-        gather_s(ot[:, m:b], win, ft[:, c + k:c + 2 * k], sem)
-
-    for i, sem in enumerate((s.gf1, s.gf2, s.gf3)):
-        a, b = CUT[i], CUT[i + 1]
-        both((T.sb, a, b), T.xs[:], (T.so, 32 * half(far) + a // 16), sem)
-    both((T.sb, CAP, 2 * CAP), T.xs[:], (T.so, 32 * half(near)), s.gn)
-
-    first, hel, nh, nea = plan(core)
-    p = first + nh * hel
-    q = p + nea
     fs, ns = slot(core, far), slot(core, near)
-
-    def direct(a, b):
-        return far, T.w[:, fs + a:fs + b], T.sb[:, a:b], s.afar, far_mask
-
-    def share(i):
-        h, a = helpers_of(core)[i], first + i * hel
-        return h, T.rl[:, 0:hel], T.sb[:, a:a + hel], s.arel, engines(inner(core)[i::2])
-
+    p = wid * (1 + nh)
+    q = p + wid
     g.wait_ge(s.gf1, 2)
-    send(direct(0, first), *[share(i) for i in range(nh)])
+    send(([far], T.w[:, fs:fs + wid], T.sb[:, 0:wid], s.afar, direct_1),
+         *[([helpers[i]], T.rl[:, 0:wid], T.sb[:, (1 + i) * wid:(2 + i) * wid], s.arel, inner(core)[i::2]) for i in range(nh)],
+         ([near], T.rl[:, 0:wid], T.sb[:, p:q], s.arel, near_share(core)))
     g.wait_ge(s.gf2, 2)
-    send((near, T.rl[:, 0:nea], T.sb[:, p:q], s.arel, near_mask))
-    g.wait_ge(s.gf3, 2)
-    send(direct(q, CAP))
+    send(([far], T.w[:, fs + q:fs + CAP], T.sb[:, q:CAP], s.afar, direct_2))
     g.wait_ge(s.gn, 2)
-    send((near, T.w[:, ns:ns + CAP], T.sb[:, CAP:2 * CAP], s.anear, near_mask))
-    first, hel, nh, nea = plan(near)
-    p = first + nh * hel
-    pass_on(near, p, p + nea, n_near)
+    send(([near], T.w[:, ns:ns + CAP], T.sb[:, CAP:2 * CAP], s.anear, inner(core)))
+    w2, nh2 = plan(near)
+    p = w2 * (1 + nh2)
+    pass_on(near, p, p + w2, len(near_share(near)))
+    g.wait_ge(s.sent, sent[0])
 
-    V.wait_ge(s.i2, 5)
-    V.wait_ge(s.lplc, 16)
-    v(V.tensor_scalar(T.ip3[:], T.ip[:], 3, None, A.arith_shift_right))
-    v(V.tensor_scalar(T.ip15[:], T.ip[:], 15, None, A.bitwise_and))
-    v(V.tensor_scalar(T.kki[:], T.pli[:], 4, None, A.arith_shift_right))
-    v(V.tensor_scalar(T.qqi[:], T.pli[:], 15, None, A.bitwise_and))
     vw()
-    v(V.tensor_scalar(T.jm[:], T.ip3[:], -1023.0, None, A.mult))
-    v(V.tensor_copy(T.p15[:], T.ip15[:]))
-    v(V.tensor_copy(T.kkf[:], T.kki[:]))
     v(V.tensor_copy(T.qqf[:], T.qqi[:]))
+    v(V.tensor_copy(T.kkf[:], T.kki[:]))
+    v(V.tensor_tensor(T.nb[:], T.neg[:], T.big[:], A.add))
     vw()
-    v(V.tensor_tensor(T.jw[:], T.jbase[:], T.jm[:], A.add))
-    v(V.tensor_scalar(T.mm[:], T.io16[:], T.p15[:, 0:1], None, A.add))
+    v(V.tensor_tensor(T.jw[:], T.jb[:], T.nb[:], A.add))
+    V.wait_ge(s.ik, 1)
+    V.wait_ge(s.tab, n_tab)
     for c in range(8):
         b = slice(128 * c, 128 * c + 128)
         V.tensor_scalar(T.ohq[:, b], T.ioq[:], T.qqf[:, c:c + 1], None, A.is_equal).then_inc(s.oh, 1)
@@ -240,21 +270,18 @@ def rank_program(g, core, T, topo):
         ins = P.matmul(T.psb[:, 0:128], T.ohq[:, b], T.ohk[:, b], c == 0, c == 7)
     ins.then_inc(s.pb, 1)
     V.wait_ge(s.pb, 1)
-    v(V.tensor_scalar(T.t1[:], T.psb[:, 0:128], 0.0, 2047.0, A.is_gt, A.mult))
+    v(V.tensor_tensor(T.offf[:], T.psb[:, 0:128], T.base[:], A.add))
     vw()
-    v(V.tensor_tensor(T.t2[:], T.t1[:], T.mm[:], A.max))
-    vw()
-    v(V.tensor_tensor(T.t3[:], T.t2[:], T.psb[:, 0:128], A.add))
-    vw()
-    V.tensor_copy(T.off[:], T.t3[:]).then_inc(s.offs, 1)
+    V.tensor_copy(T.off[:], T.offf[:]).then_inc(s.offs, 1)
 
     for e in (V, S):
         e.wait_ge(s.offs, 1)
-        e.wait_ge(s.lgh, 16)
+        e.wait_ge(s.lgh, 32)
         e.wait_ge(s.anear, n_near)
         e.wait_ge(s.afar, n_far)
     for a, b, sem in ((0, SPLIT, s.y1), (SPLIT, GC, s.y2)):
-        both((T.ys, a, b), T.w[:], (T.off, a // 16), sem)
+        m = (b - a) // 2
+        both(T.ys, a, m, m, T.w[:], T.off, a // 16, sem)
         Y.wait_ge(sem, 2)
         Y.dma_start(T.y[:, a:b], T.ys[:, a:b]).then_inc(s.st, 16)
     Y.wait_ge(s.st, 32)

from concourse.bass import DstId, RemoteDMATransfer
from concourse.mybir import AluOpType as A, ActivationFunctionType as F

CAP, TC, GC = 512, 2048, 2048
H = GC // 2
WORLD = 512
CABLE, SWITCH = (104, 2), (176, 0)
PARTS = {CABLE: ((224, 192), (64, 32)), SWITCH: ((192, 160), (96, 64))}
NEAR_V = 224
SPLIT = 640

SCRATCH = {
    "xs": ("sbuf", [128, TC], "float32"),
    "w": ("sbuf", [128, GC + 2 * CAP], "float32"),
    "ys": ("sbuf", [128, GC], "float32"),
    "sb": ("sbuf", [128, 2 * CAP], "float32"),
    "rl": ("sbuf", [128, max(CABLE[0], SWITCH[0])], "float32"),
    "negz": ("sbuf", [128, 4], "float32"),
    "li": ("sbuf", [16, 128], "int32"),
    "lf": ("sbuf", [16, 128], "float32"),
    "dq": ("sbuf", [16, 128], "float32"),
    "rep": ("sbuf", [16, 128], "float32"),
    "so": ("sbuf", [128, 64], "uint16"),
    "spr": ("sbuf", [128, 64], "float32"),
    "pick": ("sbuf", [128, 2], "uint16"),
    "pl": ("sbuf", [128, 16], "int32"),
    "kki": ("sbuf", [128, 8], "int32"),
    "qqi": ("sbuf", [128, 8], "int32"),
    "kkf": ("sbuf", [128, 8], "float32"),
    "qqf": ("sbuf", [128, 8], "float32"),
    "neg": ("sbuf", [128, 8], "float32"),
    "big": ("sbuf", [128, 8], "float32"),
    "nb": ("sbuf", [128, 8], "float32"),
    "ja": ("sbuf", [128, 8], "float32"),
    "jb": ("sbuf", [128, 8], "float32"),
    "jw": ("sbuf", [128, 8], "float32"),
    "ip": ("sbuf", [128, 4], "int32"),
    "ip4": ("sbuf", [128, 4], "int32"),
    "ipm": ("sbuf", [128, 4], "int32"),
    "jm": ("sbuf", [128, 4], "float32"),
    "g8": ("sbuf", [128, 4], "float32"),
    "pmf": ("sbuf", [128, 4], "float32"),
    "iok": ("sbuf", [128, 128], "bfloat16"),
    "ioq": ("sbuf", [128, 128], "bfloat16"),
    "io16": ("sbuf", [128, 128], "float32"),
    "base": ("sbuf", [128, 128], "float32"),
    "ohq": ("sbuf", [128, 1024], "float16"),
    "ohk": ("sbuf", [128, 1024], "float16"),
    "offf": ("sbuf", [128, 128], "float32"),
    "off": ("sbuf", [128, 128], "uint16"),
    "psa": ("psum", [128, 512], "float32"),
    "psb": ("psum", [128, 512], "float32"),
}
SEMAPHORES = ["lsnd", "lx", "lplc", "lgh", "i1", "i2", "ik", "v", "bz", "rr", "pa", "sos", "gf1", "gf2", "gn", "oh", "pb",
              "made", "offs", "sent", "tab", "afar", "arel", "anear", "y1", "y2", "st"]


def rank_program(g, core, T, topo):
    n = len(T.cores)
    s = T.sem
    V, S, P, Y = g.vector, g.scalar, g.tensor, g.sync

    def same_chip(a, b):
        return topo.host(a) == topo.host(b) and topo.chip(a) == topo.chip(b)

    ranks = [c for c in T.cores if same_chip(core, c)]
    if not ranks:
        return

    def sides(c):
        r = T.rank_of(c)
        return T.cores[(r - 1) % n], T.cores[(r + 1) % n]

    def near_of(c):
        return [d for d in sides(c) if same_chip(c, d)][0]

    def far_of(c):
        return [d for d in sides(c) if not same_chip(c, d)][0]

    def plan(c):
        return SWITCH if topo.same_plane(c, far_of(c)) else CABLE

    def owns_port(c):
        return any(topo.mates(c, m) and topo.may_write(c, m) for m in range(WORLD))

    relayed = [c for c in ranks if plan(c)[1]][0]
    own = [h for h in range(WORLD) if same_chip(h, core) and T.rank_of(h) is None and owns_port(h)]
    helpers = [[h for h in own if topo.die(h) == topo.die(relayed)][0], [h for h in own if topo.die(h) != topo.die(relayed)][0]]

    def slot(src, dst):
        return H + CAP if dst == sides(src)[0] else H

    def bits(mask):
        return [e for e in range(mask.bit_length()) if mask >> e & 1]

    def engines(es):
        return sum(1 << e for e in es)

    def addr(dst):
        rid, pid = topo.addr(dst, core)
        return DstId(rid=rid, pnc=pid)

    def outer(c):
        return bits(topo.mask(c, far_of(c)))

    def inner(c):
        return bits(topo.mask(c, near_of(c)) & ~topo.mask(c, far_of(c)))

    def near_share(c):
        return outer(c)[1::2] if plan(c)[1] else inner(c)

    sent = [0]

    def send(*ts):
        g.remote_dma_fused([RemoteDMATransfer(dst_ids=[addr(d) for d in dsts], dma_engine_mask=engines(es), remote_sem=sem,
                                              srcs=[src], dsts=[to for d in dsts])
                            for dsts, to, src, sem, es in ts], local_sem=s.sent)
        sent[0] += sum(len(t[4]) for t in ts)

    def pass_on(c, a, b, n_in):
        g.wait_ge(s.arel, n_in)
        to, at = far_of(c), slot(c, far_of(c))
        send(([to], T.w[:, at + a:at + b], T.rl[:, 0:b - a], s.afar, bits(topo.mask(core, to))))

    nv = [0]

    def v(ins):
        ins.then_inc(s.v, 1)
        nv[0] += 1

    def vw():
        V.wait_ge(s.v, nv[0])

    if T.rank_of(core) is None:
        if core not in helpers:
            return
        i = helpers.index(core)
        if i == 0:
            g.iota(T.ip[:, 0:1], [[0, 1]], 0, 1).then_inc(s.i2, 1)
            g.iota(T.io16[:], [[2 * H, 2], [16, 64]], 0, 0, allow_small_or_imprecise_dtypes=True).then_inc(s.i2, 1)
            V.wait_ge(s.i2, 2)
            v(V.tensor_scalar(T.ipm[:, 0:1], T.ip[:, 0:1], 15, None, A.bitwise_and))
            vw()
            v(V.tensor_copy(T.pmf[:, 0:1], T.ipm[:, 0:1]))
            vw()
            V.tensor_scalar(T.base[:], T.io16[:], T.pmf[:, 0:1], None, A.add).then_inc(s.made, 1)
            table = T.base
        else:
            g.iota(T.ioq[:], [[0, 8], [1, 16]], 0, 0, allow_small_or_imprecise_dtypes=True).then_inc(s.made, 1)
            table = T.ioq
        g.wait_ge(s.made, 1)
        send((ranks, table[:], table[:], s.tab, outer(relayed)))
        wid = plan(relayed)[0]
        pass_on(relayed, (1 + i) * wid, (2 + i) * wid, len(inner(relayed)[i::2]))
        g.wait_ge(s.sent, sent[0])
        return

    lo, hi = sides(core)
    near, far = near_of(core), far_of(core)
    wid, nh = plan(core)

    def half(dst):
        return 0 if dst == lo else 1

    every = bits(topo.mask(core, near))
    direct_1 = outer(core)[::2] if nh else outer(core)
    direct_2 = outer(core)
    n_near = len(inner(near))
    n_far = len(direct_1) + len(direct_2) + (1 + nh) * len(outer(core))
    n_tab = len(every) + len(helpers) * len(outer(relayed))

    S.dma_start(T.li[:, 64:128], T.plc[:]).then_inc(s.lplc, 16)
    Y.dma_start(T.li[:, 0:64], T.snd[:]).then_inc(s.lsnd, 16)
    Y.dma_start(T.xs[:], T.x[:]).then_inc(s.lx, 16)
    Y.dma_start(T.w[:, 0:H], T.gh[:, 0:H]).then_inc(s.lgh, 16)
    Y.dma_start(T.w[:, H + 2 * CAP:GC + 2 * CAP], T.gh[:, H:GC]).then_inc(s.lgh, 16)

    mine = slice(64 * ranks.index(core), 64 * ranks.index(core) + 64)
    g.iota(T.dq[:], [[0, 8], [1, 16]], 0, -1, allow_small_or_imprecise_dtypes=True).then_inc(s.i1, 1)
    g.iota(T.iok[:, mine], [[1, 64]], 64 * ranks.index(core), 0, allow_small_or_imprecise_dtypes=True).then_inc(s.ik, 1)
    g.iota(T.ja[:], [[16, 8]], H, 1, allow_small_or_imprecise_dtypes=True).then_inc(s.i2, 1)
    g.wait_ge(s.ik, 1)
    send(([near], T.iok[:, mine], T.iok[:, mine], s.tab, every))

    V.memset(T.negz[:], -0.0).then_inc(s.bz, 1)
    V.wait_ge(s.i1, 1)
    V.tensor_scalar(T.rep[:], T.dq[:], 0.0, None, A.is_equal).then_inc(s.rr, 1)
    V.wait_ge(s.i2, 1)
    v(V.tensor_scalar(T.ip[:, 0:1], T.ja[:, 0:1], -float(H), None, A.add))
    V.wait_ge(s.lsnd, 16)
    V.wait_ge(s.lplc, 16)
    V.tensor_copy(T.lf[:], T.li[:]).then_inc(s.rr, 1)

    P.wait_ge(s.rr, 2)
    P.matmul(T.psa[:, 0:128], T.rep[:], T.lf[:], True, True).then_inc(s.pa, 1)

    vw()
    v(V.tensor_scalar(T.ip4[:, 0:1], T.ip[:, 0:1], 4, None, A.arith_shift_right))
    v(V.tensor_scalar(T.ipm[:, 0:1], T.ip[:, 0:1], 7, None, A.bitwise_and))
    vw()
    v(V.tensor_scalar(T.jm[:, 0:1], T.ip4[:, 0:1], 112.0, None, A.mult))
    v(V.tensor_scalar(T.g8[:, 0:1], T.ip4[:, 0:1], 8.0, None, A.mult))
    v(V.tensor_copy(T.pmf[:, 0:1], T.ipm[:, 0:1]))
    V.wait_ge(s.pa, 1)
    V.tensor_copy(T.so[:], T.psa[:, 0:64]).then_inc(s.sos, 1)
    v(V.tensor_copy(T.spr[:], T.psa[:, 64:128]))
    vw()
    v(V.tensor_scalar(T.pick[:, 0:1], T.g8[:, 0:1], T.pmf[:, 0:1], None, A.add))
    v(V.tensor_scalar(T.jb[:], T.ja[:], T.jm[:, 0:1], None, A.add))
    vw()
    v(V.tensor_copy(T.pl[:], T.spr[:].indirect(T.pick[:, 0:1])))
    vw()
    v(V.tensor_scalar(T.kki[:], T.pl[:, 0:8], 4, None, A.arith_shift_right))
    v(V.tensor_scalar(T.qqi[:], T.pl[:, 0:8], 15, None, A.bitwise_and))
    v(V.tensor_scalar(T.neg[:], T.pl[:, 0:8], -1.0, None, A.mult))
    v(V.tensor_scalar(T.big[:], T.pl[:, 0:8], float(H), -float(H), A.is_ge, A.mult))

    V.wait_ge(s.sos, 1)
    V.wait_ge(s.lx, 16)
    S.wait_ge(s.bz, 1)
    S.wait_ge(s.sos, 1)
    S.wait_ge(s.lx, 16)

    def both(out, a, nv_, ns_, win, off, c, sem):
        k = nv_ // 16
        V.tensor_copy(out[:, a:a + nv_], win.indirect(off[:, c:c + k])).then_inc(sem, 1)
        S.activation(out[:, a + nv_:a + nv_ + ns_], win.indirect(off[:, c + k:c + k + ns_ // 16]), F.Identity,
                     bias=T.negz[:, 0:1]).then_inc(sem, 1)

    a = 0
    for (pv, ps), sem in zip(PARTS[plan(core)], (s.gf1, s.gf2)):
        both(T.sb, a, pv, ps, T.xs[:], T.so, 32 * half(far) + a // 16, sem)
        a += pv + ps
    both(T.sb, CAP, NEAR_V, CAP - NEAR_V, T.xs[:], T.so, 32 * half(near), s.gn)

    fs, ns = slot(core, far), slot(core, near)
    p = wid * (1 + nh)
    q = p + wid
    g.wait_ge(s.gf1, 2)
    send(([far], T.w[:, fs:fs + wid], T.sb[:, 0:wid], s.afar, direct_1),
         *[([helpers[i]], T.rl[:, 0:wid], T.sb[:, (1 + i) * wid:(2 + i) * wid], s.arel, inner(core)[i::2]) for i in range(nh)],
         ([near], T.rl[:, 0:wid], T.sb[:, p:q], s.arel, near_share(core)))
    g.wait_ge(s.gf2, 2)
    send(([far], T.w[:, fs + q:fs + CAP], T.sb[:, q:CAP], s.afar, direct_2))
    g.wait_ge(s.gn, 2)
    send(([near], T.w[:, ns:ns + CAP], T.sb[:, CAP:2 * CAP], s.anear, inner(core)))
    w2, nh2 = plan(near)
    p = w2 * (1 + nh2)
    pass_on(near, p, p + w2, len(near_share(near)))
    g.wait_ge(s.sent, sent[0])

    vw()
    v(V.tensor_copy(T.qqf[:], T.qqi[:]))
    v(V.tensor_copy(T.kkf[:], T.kki[:]))
    v(V.tensor_tensor(T.nb[:], T.neg[:], T.big[:], A.add))
    vw()
    v(V.tensor_tensor(T.jw[:], T.jb[:], T.nb[:], A.add))
    V.wait_ge(s.ik, 1)
    V.wait_ge(s.tab, n_tab)
    for c in range(8):
        b = slice(128 * c, 128 * c + 128)
        V.tensor_scalar(T.ohq[:, b], T.ioq[:], T.qqf[:, c:c + 1], None, A.is_equal).then_inc(s.oh, 1)
    vw()
    for c in range(8):
        b = slice(128 * c, 128 * c + 128)
        V.tensor_scalar(T.ohk[:, b], T.iok[:], T.kkf[:, c:c + 1], T.jw[:, c:c + 1], A.is_equal, A.mult).then_inc(s.oh, 1)
    P.wait_ge(s.oh, 16)
    for c in range(8):
        b = slice(128 * c, 128 * c + 128)
        ins = P.matmul(T.psb[:, 0:128], T.ohq[:, b], T.ohk[:, b], c == 0, c == 7)
    ins.then_inc(s.pb, 1)
    V.wait_ge(s.pb, 1)
    v(V.tensor_tensor(T.offf[:], T.psb[:, 0:128], T.base[:], A.add))
    vw()
    V.tensor_copy(T.off[:], T.offf[:]).then_inc(s.offs, 1)

    for e in (V, S):
        e.wait_ge(s.offs, 1)
        e.wait_ge(s.lgh, 32)
        e.wait_ge(s.anear, n_near)
        e.wait_ge(s.afar, n_far)
    for a, b, sem in ((0, SPLIT, s.y1), (SPLIT, GC, s.y2)):
        m = (b - a) // 2
        both(T.ys, a, m, m, T.w[:], T.off, a // 16, sem)
        Y.wait_ge(sem, 2)
        Y.dma_start(T.y[:, a:b], T.ys[:, a:b]).then_inc(s.st, 16)
    Y.wait_ge(s.st, 32)
